import numpy as np
import ml_dtypes


def mxq(x, axis, fmt="e4m3"):
    dtype, down = {"e4m3": (ml_dtypes.float8_e4m3fn, 7), "e5m2": (ml_dtypes.float8_e5m2, 14)}[fmt]
    v = np.moveaxis(np.asarray(x, np.float32).astype(ml_dtypes.bfloat16).astype(np.float64), axis, -1)
    blocks = v.reshape(v.shape[:-1] + (-1, 32))
    amax = np.abs(blocks).max(-1, keepdims=True)
    byte = np.maximum(np.where(amax > 0, np.frexp(amax)[1] - 1 + 127, 0) - down, 1)
    scale = np.exp2(byte - 127.0)
    codes = (blocks / scale).astype(np.float32).astype(dtype).astype(np.float64)
    return np.moveaxis((codes * scale).reshape(v.shape), -1, axis)


WIDE = False


def mx_kscale(k):
    if not WIDE:
        return np.ones(k)
    levels = np.array([10, -10, 5, -5, 0])
    if k % 512:
        return np.exp2(np.random.permutation(np.resize(levels, k // 32))).repeat(32)
    a = np.empty((k // 512, 16))
    for p in range(k // 512):
        a[p, :8] = np.random.permutation(np.resize(levels, 8))
        for g in range(8):
            far = levels[np.abs(levels - a[p, g]) >= 10]
            a[p, g + 8] = far[np.random.randint(len(far))]
    return np.exp2(a.ravel()).repeat(32)


def f64(x):
    return np.asarray(x).astype(np.float64)


def striped(idx):
    return np.tile(idx.reshape(-1, 16).T, (8, 1)).astype(np.uint16)


def unstriped(offs):
    return offs[:16].T.reshape(-1).astype(np.int64)


E2M1 = np.array([0.0, 0.5, 1.0, 1.5, 2.0, 3.0, 4.0, 6.0, -0.0, -0.5, -1.0, -1.5, -2.0, -3.0, -4.0, -6.0])


def pack_weight(w, fmt):
    k, n = w.shape
    w = f64(np.asarray(w, np.float32).astype(ml_dtypes.bfloat16)).reshape(k // 32, 32, n)
    amax = np.abs(w).max(1)
    if fmt == "e4m3":
        byte = np.frexp(amax)[1] - 1 + 127 - 7
    else:
        mant, ex = np.frexp(amax / 6.0)
        byte = np.where(mant > 0.5, ex, ex - 1) + 127
    byte = np.clip(np.where(amax > 0, byte, 1), 1, 254)
    scaled = (w * np.exp2(127.0 - byte)[:, None, :]).reshape(k, n).astype(np.float32)
    by_word = np.ascontiguousarray(scaled.reshape(k // 512, 128, 4, n).transpose(0, 1, 3, 2))
    if fmt == "e4m3":
        words = by_word.astype(ml_dtypes.float8_e4m3fn).view(np.uint8)
    else:
        c = by_word.astype(ml_dtypes.float4_e2m1fn).view(np.uint8) & 0xF
        words = (c[..., 0::2] | (c[..., 1::2] << 4)).reshape(k // 512, 128, 2 * n)
    return np.ascontiguousarray(words), np.ascontiguousarray(byte.astype(np.uint8).reshape(k // 512, 16, n))


def unpack_weight(words, scales, fmt):
    g, _, n = scales.shape
    words = np.ascontiguousarray(words).reshape(g, 128, n, -1)
    if fmt == "e4m3":
        vals = words.view(ml_dtypes.float8_e4m3fn).astype(np.float64)
    else:
        nib = np.empty((g, 128, n, 4), np.uint8)
        nib[..., 0::2] = words & 0xF
        nib[..., 1::2] = words >> 4
        vals = E2M1[nib]
    vals = vals * np.repeat(np.exp2(scales.astype(np.float64) - 127.0), 8, axis=1)[..., None]
    return vals.transpose(0, 1, 3, 2).reshape(g * 512, n)


def gelu(v):
    return 0.5 * v * (1.0 + np.tanh(np.sqrt(2.0 / np.pi) * (v + 0.044715 * v**3)))


K, T, S, H, T2, P = 1024, 2048, 512, 1024, 1024, 512

def setup_inputs():
    n = np.random.standard_normal
    s = mx_kscale(K)[:, None]
    u = mx_kscale(H)[:, None]
    d = {}
    d["tab_words"], d["tab_scales"] = pack_weight(n((K, T)) * s, "e4m3")
    d["offs"] = striped(np.random.permutation(T)[:S])
    d["w1"] = (0.8 * n((K, H)) / K ** 0.5 / s).astype(np.float32)
    d["w2_words"], d["w2_scales"] = pack_weight(0.8 * n((K, H)) / K ** 0.5 / s * u.T, "e2m1")
    d["gain"] = (np.exp(0.3 * n(H)) * u[:, 0]).astype(np.float32)
    d["wgs"] = np.exp(0.3 * n((128, S))).astype(np.float32)
    d["page0"] = (n((H, T2)) * u).astype(np.float32)
    d["offs2"] = striped(np.random.permutation(T2)[:S])
    d["offs3"] = striped(np.random.permutation(T2)[:P])
    d["cap"] = ((0.3 + 0.3 * n(H)) * u[:, 0]).astype(np.float32)
    d["vec"] = (n(H) / H ** 0.5 / u[:, 0] ** 2).astype(np.float32)
    d["slot"] = (0.8 * n(T2)).astype(np.float32)
    return d

def reference(tab_words, tab_scales, offs, w1, w2_words, w2_scales, gain, wgs, page0, offs2, offs3, cap, vec, slot):
    v = unpack_weight(tab_words, tab_scales, "e4m3")[:, unstriped(offs)]
    w2 = unpack_weight(w2_words, w2_scales, "e2m1")
    a = mxq(f64(w1), 0, "e4m3").T @ v
    b = w2.T @ v
    h = a * (b + f64(gain)[:, None]) + b
    page = f64(page0).copy()
    page[:, unstriped(offs2)] = np.tile(f64(wgs), (H // 128, 1)) * h
    x = np.minimum(page[:, unstriped(offs3)], f64(cap)[:, None]) * f64(vec)[:, None]
    e = mxq(page, 0, "e4m3").T @ mxq(x, 0, "e4m3")
    return np.abs(e - f64(slot)[:, None])

@@ -1,0 +1,321 @@
+from contextlib import ExitStack
+
+import concourse.mybir as mybir
+from concourse.masks import make_identity
+
+K, T, S, H, T2, NP = 1024, 2048, 512, 1024, 1024, 512
+P = 128
+PACK = 4
+K_PASS = P * PACK
+PASSES = 2
+TILES = H // P
+QUAD = 32
+FLOPS = 2 * (2 * K * H * S + H * T2 * NP)
+
+F32 = mybir.dt.float32
+BF16 = mybir.dt.bfloat16
+I32 = mybir.dt.int32
+U32 = mybir.dt.uint32
+U16 = mybir.dt.uint16
+U8 = mybir.dt.uint8
+FP8X4 = mybir.dt.float8_e4m3fn_x4
+FP4X4 = mybir.dt.float4_e2m1fn_x4
+ALU = mybir.AluOpType
+ACT = mybir.ActivationFunctionType
+
+W1_BLOCKS = [(0, 1), (1, 1), (2, 2), (4, 2), (6, 2)]
+W2_SPLIT = 2
+POOL_H = False
+
+
+def tile_list_guide_dog_pairing_kernel(
+    tc, tab_words, tab_scales, offs, w1, w2_words, w2_scales, gain, wgs, page0, offs2, offs3, cap, vec, slot, out
+):
+    nc = tc.nc
+    with ExitStack() as ctx:
+        keep = ctx.enter_context(tc.tile_pool(name="keep", bufs=1))
+        ring = ctx.enter_context(tc.tile_pool(name="ring", bufs=3))
+        psum = ctx.enter_context(tc.psum_pool(name="psum", bufs=4))
+
+        pick = keep.tile([P, S // 16], U16, name="pick")
+        place = keep.tile([P, S // 16], U16, name="place")
+        cand = keep.tile([P, NP // 16], U16, name="cand")
+        tab_w = [keep.tile([P, T], I32, name=f"tab_w{a}") for a in range(PASSES)]
+        tab_s = keep.tile([P, PASSES * T], U8, name="tab_s")
+        v_w = [keep.tile([P, S], U32, name=f"v_w{a}", align_bytes=64) for a in range(PASSES)]
+        v_s = [keep.tile([P, S], U8, name=f"v_s{a}", align_bytes=64) for a in range(PASSES)]
+        w1_raw = [keep.tile([P, PASSES, PACK, n * P], F32, name=f"w1_raw{t0}") for t0, n in W1_BLOCKS]
+        w2_w = [
+            keep.tile([P, PASSES, 2 * n * P], U8, name=f"w2_w{n}", align_bytes=64)
+            for n in (W2_SPLIT, TILES - W2_SPLIT)
+        ]
+        w2_s = keep.tile([P, PASSES * H], U8, name="w2_s", align_bytes=64)
+        page = [keep.tile([P, T2], F32, name=f"page{i}") for i in range(TILES)]
+        wg = keep.tile([P, S], F32, name="wg")
+        ident = keep.tile([P, P], F32, name="ident")
+        ident_bf = keep.tile([P, P], BF16, name="ident_bf")
+        gain_rows = keep.tile([P, P], F32, name="gain_rows")
+        rest_rows = keep.tile([P, P], F32, name="rest_rows")
+        gain_col = keep.tile([P, TILES], F32, name="gain_col")
+        rest_col = keep.tile([P, 3 * TILES], F32, name="rest_col")
+        page_t = [[keep.tile([P, 4, 2, P, 2], BF16, name=f"page_t{a}{h}") for h in range(2)] for a in range(PASSES)]
+        x_t = [keep.tile([P, 4, 2, P], F32, name=f"x_t{a}") for a in range(PASSES)]
+        page_w = [keep.tile([P, T2], U32, name=f"page_w{a}", align_bytes=64) for a in range(PASSES)]
+        page_s = [keep.tile([P, T2], U8, name=f"page_s{a}", align_bytes=64) for a in range(PASSES)]
+        x_w = [keep.tile([P, NP], U32, name=f"x_w{a}", align_bytes=64) for a in range(PASSES)]
+        x_s = [keep.tile([P, NP], U8, name=f"x_s{a}", align_bytes=64) for a in range(PASSES)]
+
+        def load_scales(queue, plane, scales):
+            rows = scales.bitcast(I32)
+            for q in range(4):
+                queue.dma_start(
+                    out=plane[QUAD * q : QUAD * q + 4, :].bitcast(I32).rearrange("r (a c) -> r a c", a=PASSES),
+                    in_=rows[:, 4 * q : 4 * q + 4, :].rearrange("a r c -> r a c"),
+                )
+
+        def load_table(a):
+            nc.sync.dma_start(out=tab_w[a][:], in_=tab_words[a].rearrange("p t i -> p (t i)").bitcast(I32))
+
+        def load_w1(blk):
+            t0, n = W1_BLOCKS[blk]
+            for a in range(PASSES):
+                rows = w1[a * K_PASS : (a + 1) * K_PASS, t0 * P : (t0 + n) * P]
+                nc.sync.dma_start(out=w1_raw[blk][:, a, :, :], in_=rows.rearrange("(p j) c -> p j c", j=PACK))
+
+        def load_w2(part):
+            c0, c1 = ((0, W2_SPLIT), (W2_SPLIT, TILES))[part]
+            words = w2_words.bitcast(I32)[:, :, c0 * P // 2 : c1 * P // 2]
+            nc.sync.dma_start(out=w2_w[part][:].bitcast(I32), in_=words.rearrange("a p c -> p a c"))
+
+        def load_page(i):
+            nc.sync.dma_start(out=page[i][:], in_=page0[i * P : (i + 1) * P, :])
+
+        nc.vector.memset(tab_s[:].bitcast(I32), 0)
+        nc.vector.memset(w2_s[:].bitcast(I32), 0)
+        nc.vector.memset(gain_rows[:], 0.0)
+        nc.vector.memset(rest_rows[:], 0.0)
+        make_identity(nc, ident[:])
+        nc.vector.tensor_copy(out=ident_bf[:], in_=ident[:])
+
+        nc.sync.dma_start(pick[:], offs)
+        load_table(0)
+        load_scales(nc.scalar, tab_s, tab_scales)
+        load_w1(0)
+        load_table(1)
+        load_w2(0)
+        load_scales(nc.sync, w2_s, w2_scales)
+        nc.sync.dma_start(out=gain_rows[0:TILES, :], in_=gain.rearrange("(i p) -> i p", p=P))
+        load_page(0)
+        nc.sync.dma_start(place[:], offs2)
+        nc.sync.dma_start(out=wg[:], in_=wgs)
+        load_w1(1)
+        nc.sync.dma_start(cand[:], offs3)
+        for n, v in enumerate((cap, vec, slot)):
+            nc.sync.dma_start(out=rest_rows[n * TILES : (n + 1) * TILES, :], in_=v.rearrange("(i p) -> i p", p=P))
+        load_w2(1)
+        load_w1(2)
+        load_page(1)
+        load_w1(3)
+        load_page(2)
+        load_w1(4)
+        for i in range(3, TILES):
+            load_page(i)
+
+        def spread(rows, cols):
+            bank = psum.tile([P, P], F32, name="spread", tag="turn")
+            nc.tensor.transpose(bank[:], rows[:], ident[:])
+            nc.scalar.copy(out=cols[:], in_=bank[:, 0 : cols.shape[1]])
+
+        w1_q = {}
+        readings = {}
+        revised = {}
+        picked = {}
+
+        def quantise_w1(i):
+            blk = max(n for n, (t0, cnt) in enumerate(W1_BLOCKS) if t0 <= i)
+            c0 = (i - W1_BLOCKS[blk][0]) * P
+            grouped = ring.tile([P, PASSES, P, PACK], BF16, name="grouped", align_bytes=64)
+            nc.scalar.copy(
+                out=grouped[:].rearrange("p a (c i) t -> p a c t i", i=4),
+                in_=w1_raw[blk][:, :, :, c0 : c0 + P].rearrange("p a t (c i) -> p a c t i", i=4),
+            )
+            codes = ring.tile([P, PASSES * P], U32, name="w1_w", align_bytes=64)
+            scales = ring.tile([P, PASSES * P], U8, name="w1_s", align_bytes=64)
+            nc.vector.quantize_mx(
+                out=codes[:].bitcast(FP8X4), scales=scales[:], in_=grouped[:].rearrange("p a c t -> p (a c t)")
+            )
+            w1_q[i] = (codes, scales)
+
+        def read_table(i):
+            codes, scales = w1_q[i]
+            part, c0 = (0, i * P) if i < W2_SPLIT else (1, (i - W2_SPLIT) * P)
+            b_bank = psum.tile([P, S], F32, name="b_bank", tag="sum")
+            a_bank = psum.tile([P, S], F32, name="a_bank", tag="sum")
+            for a in range(PASSES):
+                nc.tensor.matmul_mx(
+                    out=b_bank[:],
+                    lhsT=w2_w[part][:, a, 2 * c0 : 2 * (c0 + P)].bitcast(FP4X4),
+                    lhsT_scale=w2_s[:, a * H + i * P : a * H + (i + 1) * P],
+                    rhs=v_w[a][:].bitcast(FP8X4),
+                    rhs_scale=v_s[a][:],
+                    start=(a == 0),
+                    stop=(a == PASSES - 1),
+                )
+            for a in range(PASSES):
+                nc.tensor.matmul_mx(
+                    out=a_bank[:],
+                    lhsT=codes[:, a * P : (a + 1) * P].bitcast(FP8X4),
+                    lhsT_scale=scales[:, a * P : (a + 1) * P],
+                    rhs=v_w[a][:].bitcast(FP8X4),
+                    rhs_scale=v_s[a][:],
+                    start=(a == 0),
+                    stop=(a == PASSES - 1),
+                )
+            b_sb = ring.tile([P, S], F32, name="b_sb")
+            nc.scalar.copy(out=b_sb[:], in_=b_bank[:])
+            readings[i] = (a_bank, b_sb)
+
+        def combine(i):
+            a_bank, b_sb = readings[i]
+            prod = ring.tile([P, S], F32, name="prod")
+            nc.vector.scalar_tensor_tensor(
+                out=prod[:], in0=b_sb[:], scalar=gain_col[:, i : i + 1], in1=a_bank[:], op0=ALU.add, op1=ALU.mult
+            )
+            h = ring.tile([P, S], F32, name="h")
+            if POOL_H and i > 0:
+                nc.gpsimd.tensor_tensor(out=h[:], in0=prod[:], in1=b_sb[:], op=ALU.add)
+                hw = ring.tile([P, S], F32, name="hw")
+                nc.gpsimd.tensor_tensor(out=hw[:], in0=h[:], in1=wg[:], op=ALU.mult)
+                revised[i] = hw
+            else:
+                nc.vector.tensor_tensor(out=h[:], in0=prod[:], in1=b_sb[:], op=ALU.add)
+                revised[i] = h
+
+        def scatter(i):
+            if POOL_H and i > 0:
+                nc.vector.tensor_copy(out=page[i][:].indirect(place[:]), in_=revised[i][:])
+            else:
+                nc.vector.tensor_tensor(out=page[i][:].indirect(place[:]), in0=revised[i][:], in1=wg[:], op=ALU.mult)
+
+        def gather(i):
+            g = ring.tile([P, NP], F32, name="g")
+            nc.vector.tensor_copy(out=g[:], in_=page[i][:].indirect(cand[:]))
+            picked[i] = g
+
+        def turn_page(i):
+            a, q = divmod(i, 4)
+            for half in range(2):
+                bank = psum.tile([P, 4, P], F32, name="page_turn", tag="turn")
+                for j in range(4):
+                    m0 = (4 * half + j) * P
+                    nc.tensor.transpose(bank[:, j, :], page[i][:, m0 : m0 + P], ident[:])
+                nc.scalar.copy(
+                    out=page_t[a][half][:, :, :, QUAD * q : QUAD * (q + 1), :],
+                    in_=bank[:].rearrange("m j (p u e) -> m j u p e", u=2, e=2),
+                )
+
+        def turn_x(i):
+            a, q = divmod(i, 4)
+            x = ring.tile([P, NP], BF16, name="x")
+            nc.vector.tensor_scalar(
+                out=x[:],
+                in0=picked[i][:],
+                scalar1=rest_col[:, i : i + 1],
+                scalar2=rest_col[:, TILES + i : TILES + i + 1],
+                op0=ALU.min,
+                op1=ALU.mult,
+            )
+            bank = psum.tile([P, 4, P], BF16, name="x_turn", tag="turn")
+            for j in range(4):
+                nc.tensor.transpose(bank[:, j, :], x[:, j * P : (j + 1) * P], ident_bf[:])
+            move = nc.vector.tensor_copy if i == TILES - 1 else nc.scalar.copy
+            move(
+                out=x_t[a][:, :, :, QUAD * q : QUAD * (q + 1)],
+                in_=bank[:].bitcast(F32).rearrange("n j (p u) -> n j u p", u=2),
+            )
+
+        def turn_back(pairs, codes, scales, move):
+            bank = psum.tile([P, 2, 2, P], F32, name="back", tag="turn")
+            for j in range(2):
+                for u in range(2):
+                    nc.tensor.transpose(bank[:, j, u, :], pairs[:, j, u, :], ident[:])
+            woven = ring.tile([P, 2, P, 2], F32, name="woven", align_bytes=64)
+            move(out=woven[:], in_=bank[:].rearrange("p j u m -> p j m u"))
+            nc.vector.quantize_mx(
+                out=codes.bitcast(FP8X4), scales=scales, in_=woven[:].rearrange("p j m u -> p (j m u)").bitcast(BF16)
+            )
+
+        def quantise_x(a):
+            for jj in range(2):
+                cols = slice(2 * jj * P, 2 * (jj + 1) * P)
+                turn_back(x_t[a][:, 2 * jj : 2 * jj + 2, :, :], x_w[a][:, cols], x_s[a][:, cols], nc.vector.tensor_copy if a == 1 else nc.scalar.copy)
+
+        def quantise_page(a, jj):
+            half, lo = divmod(2 * jj, 4)
+            words = page_t[a][half][:].rearrange("m j u p e -> m j u (p e)").bitcast(F32)
+            cols = slice(2 * jj * P, 2 * (jj + 1) * P)
+            turn_back(words[:, lo : lo + 2, :, :], page_w[a][:, cols], page_s[a][:, cols], nc.vector.tensor_copy if a == 1 and jj >= 2 else nc.scalar.copy)
+
+        e_banks = {}
+
+        def compare(j, passes):
+            cols = slice(j * P, (j + 1) * P)
+            if j not in e_banks:
+                e_banks[j] = psum.tile([P, NP], F32, name="e_bank", tag="sum")
+            bank = e_banks[j]
+            for a in passes:
+                nc.tensor.matmul_mx(
+                    out=bank[:],
+                    lhsT=page_w[a][:, cols].bitcast(FP8X4),
+                    lhsT_scale=page_s[a][:, cols],
+                    rhs=x_w[a][:].bitcast(FP8X4),
+                    rhs_scale=x_s[a][:],
+                    start=(a == 0),
+                    stop=(a == PASSES - 1),
+                )
+            if 1 not in passes:
+                return
+            dist = ring.tile([P, NP], F32, name="dist", bufs=4)
+            nc.scalar.activation(
+                out=dist[:], in_=bank[:], func=ACT.Abs, bias=rest_col[:, 2 * TILES + j : 2 * TILES + j + 1], scale=-1.0
+            )
+            nc.sync.dma_start(out=out[cols, :], in_=dist[:])
+
+        spread(gain_rows, gain_col)
+        for a in range(PASSES):
+            nc.vector.tensor_copy(out=v_s[a][:], in_=tab_s[:, a * T : (a + 1) * T].indirect(pick[:]))
+        nc.vector.tensor_copy(out=v_w[0][:], in_=tab_w[0][:].bitcast(U32).indirect(pick[:]))
+        quantise_w1(0)
+        nc.vector.tensor_copy(out=v_w[1][:], in_=tab_w[1][:].bitcast(U32).indirect(pick[:]))
+        read_table(0)
+        quantise_w1(1)
+        combine(0)
+        spread(rest_rows, rest_col)
+        read_table(1)
+        for i in range(TILES):
+            if i + 2 < TILES:
+                quantise_w1(i + 2)
+            if i + 1 < TILES:
+                combine(i + 1)
+            if i + 2 < TILES:
+                read_table(i + 2)
+            scatter(i)
+            if i > 0:
+                turn_x(i - 1)
+            gather(i)
+            turn_page(i)
+            if i == 4:
+                quantise_x(0)
+            if 4 <= i < 6:
+                quantise_page(0, 2 * (i - 4))
+                quantise_page(0, 2 * (i - 4) + 1)
+        for j in range(4):
+            compare(j, [0])
+        turn_x(TILES - 1)
+        quantise_page(1, 0)
+        quantise_x(1)
+        for jj in range(4):
+            if jj + 1 < 4:
+                quantise_page(1, jj + 1)
+            for j in (2 * jj, 2 * jj + 1):
+                compare(j, [1] if j < 4 else [0, 1])

@@ -10,6 +10,8 @@ K_PASS = P * PACK
 PASSES = 2
 TILES = H // P
 QUAD = 32
+CHUNK = 256
+RUN = 8
 FLOPS = 2 * (2 * K * H * S + H * T2 * NP)
 
 F32 = mybir.dt.float32
@@ -23,9 +25,7 @@ FP4X4 = mybir.dt.float4_e2m1fn_x4
 ALU = mybir.AluOpType
 ACT = mybir.ActivationFunctionType
 
-W1_BLOCKS = [(0, 1), (1, 1), (2, 2), (4, 2), (6, 2)]
-W2_SPLIT = 2
-POOL_H = False
+ROW = 4 * S
 
 
 def tile_list_guide_dog_pairing_kernel(
@@ -34,7 +34,8 @@ def tile_list_guide_dog_pairing_kernel(
     nc = tc.nc
     with ExitStack() as ctx:
         keep = ctx.enter_context(tc.tile_pool(name="keep", bufs=1))
-        ring = ctx.enter_context(tc.tile_pool(name="ring", bufs=3))
+        reuse = ctx.enter_context(tc.tile_pool(name="reuse", bufs=1))
+        ring = ctx.enter_context(tc.tile_pool(name="ring", bufs=4))
         psum = ctx.enter_context(tc.psum_pool(name="psum", bufs=4))
 
         pick = keep.tile([P, S // 16], U16, name="pick")
@@ -44,118 +45,172 @@ def tile_list_guide_dog_pairing_kernel(
         tab_s = keep.tile([P, PASSES * T], U8, name="tab_s")
         v_w = [keep.tile([P, S], U32, name=f"v_w{a}", align_bytes=64) for a in range(PASSES)]
         v_s = [keep.tile([P, S], U8, name=f"v_s{a}", align_bytes=64) for a in range(PASSES)]
-        w1_raw = [keep.tile([P, PASSES, PACK, n * P], F32, name=f"w1_raw{t0}") for t0, n in W1_BLOCKS]
-        w2_w = [
-            keep.tile([P, PASSES, 2 * n * P], U8, name=f"w2_w{n}", align_bytes=64)
-            for n in (W2_SPLIT, TILES - W2_SPLIT)
-        ]
-        w2_s = keep.tile([P, PASSES * H], U8, name="w2_s", align_bytes=64)
+        w1_blocks = [(0, P), (P, P), (2 * P, 2 * P), (K_PASS, K_PASS)]
+        w1_raw = [keep.tile([P, PASSES, PACK, n], F32, name=f"w1_raw{c0}") for c0, n in w1_blocks]
+        w2_w = [keep.tile([P, PASSES, K_PASS // 2], I32, name=f"w2_w{n}", align_bytes=64) for n in range(2)]
+        w2_s = keep.tile([P, PASSES, H // 4], I32, name="w2_s", align_bytes=64)
+        w2_w_dealt = keep.tile([P, PASSES, PACK, P // 2], I32, name="w2_w_dealt", align_bytes=64)
+        w2_s_dealt = keep.tile([P, PASSES, PACK, P // 4], I32, name="w2_s_dealt", align_bytes=64)
         page = [keep.tile([P, T2], F32, name=f"page{i}") for i in range(TILES)]
         wg = keep.tile([P, S], F32, name="wg")
+        wg_dealt = keep.tile([P, PACK, S], F32, name="wg_dealt")
         ident = keep.tile([P, P], F32, name="ident")
         ident_bf = keep.tile([P, P], BF16, name="ident_bf")
         gain_rows = keep.tile([P, P], F32, name="gain_rows")
         rest_rows = keep.tile([P, P], F32, name="rest_rows")
-        gain_col = keep.tile([P, TILES], F32, name="gain_col")
-        rest_col = keep.tile([P, 3 * TILES], F32, name="rest_col")
-        page_t = [[keep.tile([P, 4, 2, P, 2], BF16, name=f"page_t{a}{h}") for h in range(2)] for a in range(PASSES)]
-        x_t = [keep.tile([P, 4, 2, P], F32, name=f"x_t{a}") for a in range(PASSES)]
-        page_w = [keep.tile([P, T2], U32, name=f"page_w{a}", align_bytes=64) for a in range(PASSES)]
+        gain_col = keep.tile([P, PACK], F32, name="gain_col")
+        rest_col = keep.tile([P, 2 * PACK + TILES], F32, name="rest_col")
+        dealt_rows = keep.tile([P, P], F32, name="dealt_rows")
+        dealt_col = keep.tile([P, 3 * PACK], F32, name="dealt_col")
+        page_t = [reuse.tile([P, 4, 2, P, 2], BF16, name=f"page_t{h}", offset=(18 + 2 * h) * ROW) for h in range(2)]
+        x_t = reuse.tile([P, 4, 2, P], F32, name="x_t", offset=22 * ROW)
+        page_bf = [
+            reuse.tile([P, CHUNK, PACK], BF16, name=f"page_bf{c}", align_bytes=64, offset=(23 - c) * ROW)
+            for c in range(T2 // CHUNK)
+        ]
+        x_bf = keep.tile([P, NP, PACK], BF16, name="x_bf", align_bytes=64)
         page_s = [keep.tile([P, T2], U8, name=f"page_s{a}", align_bytes=64) for a in range(PASSES)]
-        x_w = [keep.tile([P, NP], U32, name=f"x_w{a}", align_bytes=64) for a in range(PASSES)]
         x_s = [keep.tile([P, NP], U8, name=f"x_s{a}", align_bytes=64) for a in range(PASSES)]
 
-        def load_scales(queue, plane, scales):
+        w1_bf = [keep.tile([P, PASSES, P, PACK], BF16, name=f"w1_bf{i}", align_bytes=64) for i in range(TILES)]
+        weighted_at = [i * ROW for i in range(5)] + [6 * ROW, 9 * ROW, 10 * ROW]
+        codes_at = [11 * ROW + i * ROW // 2 for i in range(3)] + weighted_at[:5]
+        picked_at = [(13 + 2 * (i % 2)) * ROW for i in range(TILES)]
+        woven = keep.tile([P, 6, 2, P, 2], F32, name="woven", align_bytes=64)
+        x_w = [None, keep.tile([P, NP], U32, name="x_w1", align_bytes=64)]
+        page_w = [None, keep.tile([P, T2], U32, name="page_w1", align_bytes=64)]
+
+        def load_scales(plane, scales):
             rows = scales.bitcast(I32)
             for q in range(4):
-                queue.dma_start(
-                    out=plane[QUAD * q : QUAD * q + 4, :].bitcast(I32).rearrange("r (a c) -> r a c", a=PASSES),
-                    in_=rows[:, 4 * q : 4 * q + 4, :].rearrange("a r c -> r a c"),
+                nc.sync.dma_start(
+                    out=plane[QUAD * q : QUAD * q + 4], in_=rows[:, 4 * q : 4 * q + 4, :].rearrange("a r c -> r a c")
                 )
 
         def load_table(a):
             nc.sync.dma_start(out=tab_w[a][:], in_=tab_words[a].rearrange("p t i -> p (t i)").bitcast(I32))
 
         def load_w1(blk):
-            t0, n = W1_BLOCKS[blk]
+            c0, n = w1_blocks[blk]
             for a in range(PASSES):
-                rows = w1[a * K_PASS : (a + 1) * K_PASS, t0 * P : (t0 + n) * P]
+                rows = w1[a * K_PASS : (a + 1) * K_PASS, c0 : c0 + n]
                 nc.sync.dma_start(out=w1_raw[blk][:, a, :, :], in_=rows.rearrange("(p j) c -> p j c", j=PACK))
 
-        def load_w2(part):
-            c0, c1 = ((0, W2_SPLIT), (W2_SPLIT, TILES))[part]
-            words = w2_words.bitcast(I32)[:, :, c0 * P // 2 : c1 * P // 2]
-            nc.sync.dma_start(out=w2_w[part][:].bitcast(I32), in_=words.rearrange("a p c -> p a c"))
+        def load_w2(n):
+            words = w2_words.bitcast(I32).rearrange("a p (n c) -> n p a c", n=2)
+            nc.sync.dma_start(out=w2_w[n][:], in_=words[n])
 
         def load_page(i):
-            nc.sync.dma_start(out=page[i][:], in_=page0[i * P : (i + 1) * P, :])
+            if i < PACK:
+                rows = page0[i * P : (i + 1) * P, :]
+            else:
+                rows = page0[K_PASS:, :].rearrange("(g t i) m -> t g i m", t=PACK, i=RUN)[i - PACK]
+            nc.sync.dma_start(out=page[i][:], in_=rows)
 
-        nc.vector.memset(tab_s[:].bitcast(I32), 0)
-        nc.vector.memset(w2_s[:].bitcast(I32), 0)
+        nc.gpsimd.memset(tab_s[:].bitcast(I32), 0)
+        nc.vector.memset(w2_s[:], 0)
         nc.vector.memset(gain_rows[:], 0.0)
         nc.vector.memset(rest_rows[:], 0.0)
+        nc.vector.memset(dealt_rows[:], 0.0)
         make_identity(nc, ident[:])
         nc.vector.tensor_copy(out=ident_bf[:], in_=ident[:])
 
         nc.sync.dma_start(pick[:], offs)
         load_table(0)
-        load_scales(nc.scalar, tab_s, tab_scales)
+        load_scales(tab_s[:].bitcast(I32).rearrange("p (a c) -> p a c", a=PASSES), tab_scales)
         load_w1(0)
         load_table(1)
+        load_scales(w2_s[:], w2_scales)
         load_w2(0)
-        load_scales(nc.sync, w2_s, w2_scales)
-        nc.sync.dma_start(out=gain_rows[0:TILES, :], in_=gain.rearrange("(i p) -> i p", p=P))
+        nc.sync.dma_start(out=gain_rows[0:PACK, :], in_=gain[:K_PASS].rearrange("(i p) -> i p", p=P))
+        load_w1(1)
         load_page(0)
         nc.sync.dma_start(place[:], offs2)
         nc.sync.dma_start(out=wg[:], in_=wgs)
-        load_w1(1)
-        nc.sync.dma_start(cand[:], offs3)
-        for n, v in enumerate((cap, vec, slot)):
-            nc.sync.dma_start(out=rest_rows[n * TILES : (n + 1) * TILES, :], in_=v.rearrange("(i p) -> i p", p=P))
-        load_w2(1)
         load_w1(2)
-        load_page(1)
+        nc.sync.dma_start(cand[:], offs3)
+        for n, v in enumerate((cap[:K_PASS], vec[:K_PASS], slot)):
+            rows = v.rearrange("(i p) -> i p", p=P)
+            nc.sync.dma_start(out=rest_rows[n * PACK : n * PACK + rows.shape[0], :], in_=rows)
         load_w1(3)
+        load_page(1)
+        load_w2(1)
+        for n, v in enumerate((gain, cap, vec)):
+            rows = v[K_PASS:].rearrange("(g t i) -> t g i", t=PACK, i=RUN)
+            nc.sync.dma_start(out=dealt_rows[n * PACK : (n + 1) * PACK, :].rearrange("t (g i) -> t g i", i=RUN), in_=rows)
         load_page(2)
-        load_w1(4)
-        for i in range(3, TILES):
-            load_page(i)
+        load_page(3)
+        for t in range(PACK):
+            for q in range(4):
+                rows = wgs.rearrange("(g t i) j -> t g i j", t=PACK, i=RUN)[t]
+                nc.sync.dma_start(out=wg_dealt[QUAD * q : QUAD * (q + 1), t, :], in_=rows)
+            load_page(PACK + t)
 
         def spread(rows, cols):
             bank = psum.tile([P, P], F32, name="spread", tag="turn")
             nc.tensor.transpose(bank[:], rows[:], ident[:])
             nc.scalar.copy(out=cols[:], in_=bank[:, 0 : cols.shape[1]])
 
+        def column(n, i):
+            if i >= PACK:
+                c = (n - 1) * PACK + i
+                return dealt_col[:, c : c + 1]
+            if n == 0:
+                return gain_col[:, i : i + 1]
+            return rest_col[:, (n - 1) * PACK + i : (n - 1) * PACK + i + 1]
+
         w1_q = {}
         readings = {}
         revised = {}
         picked = {}
+        e_banks = {}
+
+        def round_w1(i):
+            if i < PACK:
+                blk = min(i, 2)
+                c0 = i * P - w1_blocks[blk][0]
+                nc.scalar.copy(
+                    out=w1_bf[i][:].rearrange("p a (c i) j -> p a c j i", i=4),
+                    in_=w1_raw[blk][:, :, :, c0 : c0 + P].rearrange("p a j (c i) -> p a c j i", i=4),
+                )
+            else:
+                nc.scalar.copy(
+                    out=w1_bf[i][:].rearrange("p a (g i) j -> p a g j i", i=RUN),
+                    in_=w1_raw[3][:].rearrange("p a j (g t i) -> p t a g j i", t=PACK, i=RUN)[:, i - PACK],
+                )
+
+        def deal_w2():
+            nc.vector.tensor_copy(
+                out=w2_w_dealt[:].rearrange("p a t (g w) -> p a t g w", w=RUN // 2),
+                in_=w2_w[1][:].rearrange("p a (g t w) -> p a t g w", t=PACK, w=RUN // 2),
+            )
+            nc.vector.tensor_copy(
+                out=w2_s_dealt[:].rearrange("p a t (g w) -> p a t g w", w=RUN // 4),
+                in_=w2_s[:, :, K_PASS // 4 :].rearrange("p a (g t w) -> p a t g w", t=PACK, w=RUN // 4),
+            )
 
         def quantise_w1(i):
-            blk = max(n for n, (t0, cnt) in enumerate(W1_BLOCKS) if t0 <= i)
-            c0 = (i - W1_BLOCKS[blk][0]) * P
-            grouped = ring.tile([P, PASSES, P, PACK], BF16, name="grouped", align_bytes=64)
-            nc.scalar.copy(
-                out=grouped[:].rearrange("p a (c i) t -> p a c t i", i=4),
-                in_=w1_raw[blk][:, :, :, c0 : c0 + P].rearrange("p a t (c i) -> p a c t i", i=4),
-            )
-            codes = ring.tile([P, PASSES * P], U32, name="w1_w", align_bytes=64)
+            rounded = w1_bf[i][:]
+            codes = reuse.tile([P, PASSES * P], U32, name=f"w1_w{i}", align_bytes=64, offset=codes_at[i])
             scales = ring.tile([P, PASSES * P], U8, name="w1_s", align_bytes=64)
             nc.vector.quantize_mx(
-                out=codes[:].bitcast(FP8X4), scales=scales[:], in_=grouped[:].rearrange("p a c t -> p (a c t)")
+                out=codes[:].bitcast(FP8X4), scales=scales[:], in_=rounded.rearrange("p a c j -> p (a c j)")
             )
             w1_q[i] = (codes, scales)
 
         def read_table(i):
             codes, scales = w1_q[i]
-            part, c0 = (0, i * P) if i < W2_SPLIT else (1, (i - W2_SPLIT) * P)
-            b_bank = psum.tile([P, S], F32, name="b_bank", tag="sum")
-            a_bank = psum.tile([P, S], F32, name="a_bank", tag="sum")
+            a_bank = psum.tile([P, S], F32, name="a_bank", tag="first", bufs=2)
+            b_bank = psum.tile([P, S], F32, name="b_bank", tag="second", bufs=2)
             for a in range(PASSES):
+                if i < PACK:
+                    words, plane = w2_w[0][:, a, i * P // 2 : (i + 1) * P // 2], w2_s[:, a, i * P // 4 : (i + 1) * P // 4]
+                else:
+                    words, plane = w2_w_dealt[:, a, i - PACK], w2_s_dealt[:, a, i - PACK]
                 nc.tensor.matmul_mx(
                     out=b_bank[:],
-                    lhsT=w2_w[part][:, a, 2 * c0 : 2 * (c0 + P)].bitcast(FP4X4),
-                    lhsT_scale=w2_s[:, a * H + i * P : a * H + (i + 1) * P],
+                    lhsT=words.bitcast(FP4X4),
+                    lhsT_scale=plane.bitcast(U8),
                     rhs=v_w[a][:].bitcast(FP8X4),
                     rhs_scale=v_s[a][:],
                     start=(a == 0),
@@ -171,97 +226,93 @@ def tile_list_guide_dog_pairing_kernel(
                     start=(a == 0),
                     stop=(a == PASSES - 1),
                 )
-            b_sb = ring.tile([P, S], F32, name="b_sb")
+            b_sb = ring.tile([P, S], F32, name="b_sb", bufs=3)
             nc.scalar.copy(out=b_sb[:], in_=b_bank[:])
-            readings[i] = (a_bank, b_sb)
+            if i == 0:
+                readings[i] = (a_bank, b_sb)
+                return
+            b_gain = ring.tile([P, S], F32, name="b_gain", bufs=3)
+            nc.scalar.activation(out=b_gain[:], in_=b_bank[:], func=ACT.Identity, bias=column(0, i))
+            a_sb = ring.tile([P, S], F32, name="a_sb", bufs=3)
+            nc.scalar.copy(out=a_sb[:], in_=a_bank[:])
+            readings[i] = (a_sb, b_sb, b_gain)
+
+        def weights(i):
+            return wg[:] if i < PACK else wg_dealt[:, i - PACK]
 
         def combine(i):
-            a_bank, b_sb = readings[i]
-            prod = ring.tile([P, S], F32, name="prod")
-            nc.vector.scalar_tensor_tensor(
-                out=prod[:], in0=b_sb[:], scalar=gain_col[:, i : i + 1], in1=a_bank[:], op0=ALU.add, op1=ALU.mult
-            )
-            h = ring.tile([P, S], F32, name="h")
-            if POOL_H and i > 0:
-                nc.gpsimd.tensor_tensor(out=h[:], in0=prod[:], in1=b_sb[:], op=ALU.add)
-                hw = ring.tile([P, S], F32, name="hw")
-                nc.gpsimd.tensor_tensor(out=hw[:], in0=h[:], in1=wg[:], op=ALU.mult)
-                revised[i] = hw
-            else:
+            prod = reuse.tile([P, S], F32, name=f"prod{i}", offset=picked_at[i] + ROW // 2)
+            h = reuse.tile([P, S], F32, name=f"h{i}", offset=picked_at[i - 1] + ROW)
+            revised[i] = reuse.tile([P, S], F32, name=f"weighted{i}", offset=weighted_at[i])[:]
+            if i == 0:
+                a_bank, b_sb = readings[i]
+                nc.vector.scalar_tensor_tensor(
+                    out=prod[:], in0=b_sb[:], scalar=column(0, i), in1=a_bank[:], op0=ALU.add, op1=ALU.mult
+                )
                 nc.vector.tensor_tensor(out=h[:], in0=prod[:], in1=b_sb[:], op=ALU.add)
-                revised[i] = h
+                nc.vector.tensor_tensor(out=revised[i], in0=h[:], in1=weights(i), op=ALU.mult)
+                return
+            a_sb, b_sb, b_gain = readings[i]
+            nc.gpsimd.tensor_tensor(out=prod[:], in0=a_sb[:], in1=b_gain[:], op=ALU.mult)
+            nc.gpsimd.tensor_tensor(out=h[:], in0=prod[:], in1=b_sb[:], op=ALU.add)
+            nc.gpsimd.tensor_tensor(out=revised[i], in0=h[:], in1=weights(i), op=ALU.mult)
 
         def scatter(i):
-            if POOL_H and i > 0:
-                nc.vector.tensor_copy(out=page[i][:].indirect(place[:]), in_=revised[i][:])
-            else:
-                nc.vector.tensor_tensor(out=page[i][:].indirect(place[:]), in0=revised[i][:], in1=wg[:], op=ALU.mult)
+            nc.vector.tensor_copy(out=page[i][:].indirect(place[:]), in_=revised[i])
 
         def gather(i):
-            g = ring.tile([P, NP], F32, name="g")
-            nc.vector.tensor_copy(out=g[:], in_=page[i][:].indirect(cand[:]))
-            picked[i] = g
+            picked[i] = reuse.tile([P, NP], F32, name=f"picked{i}", offset=picked_at[i])[:]
+            nc.vector.tensor_copy(out=picked[i], in_=page[i][:].indirect(cand[:]))
+
+        def cap_x(i, x):
+            nc.vector.tensor_scalar(
+                out=x, in0=picked[i], scalar1=column(1, i), scalar2=column(2, i), op0=ALU.min, op1=ALU.mult
+            )
 
         def turn_page(i):
-            a, q = divmod(i, 4)
             for half in range(2):
                 bank = psum.tile([P, 4, P], F32, name="page_turn", tag="turn")
                 for j in range(4):
                     m0 = (4 * half + j) * P
                     nc.tensor.transpose(bank[:, j, :], page[i][:, m0 : m0 + P], ident[:])
                 nc.scalar.copy(
-                    out=page_t[a][half][:, :, :, QUAD * q : QUAD * (q + 1), :],
+                    out=page_t[half][:, :, :, QUAD * i : QUAD * (i + 1), :],
                     in_=bank[:].rearrange("m j (p u e) -> m j u p e", u=2, e=2),
                 )
 
         def turn_x(i):
-            a, q = divmod(i, 4)
-            x = ring.tile([P, NP], BF16, name="x")
-            nc.vector.tensor_scalar(
-                out=x[:],
-                in0=picked[i][:],
-                scalar1=rest_col[:, i : i + 1],
-                scalar2=rest_col[:, TILES + i : TILES + i + 1],
-                op0=ALU.min,
-                op1=ALU.mult,
-            )
+            x = ring.tile([P, NP], BF16, name="x", bufs=2)
+            cap_x(i, x[:])
             bank = psum.tile([P, 4, P], BF16, name="x_turn", tag="turn")
             for j in range(4):
                 nc.tensor.transpose(bank[:, j, :], x[:, j * P : (j + 1) * P], ident_bf[:])
-            move = nc.vector.tensor_copy if i == TILES - 1 else nc.scalar.copy
-            move(
-                out=x_t[a][:, :, :, QUAD * q : QUAD * (q + 1)],
+            nc.scalar.copy(
+                out=x_t[:, :, :, QUAD * i : QUAD * (i + 1)],
                 in_=bank[:].bitcast(F32).rearrange("n j (p u) -> n j u p", u=2),
             )
 
-        def turn_back(pairs, codes, scales, move):
+        def turn_back(pairs, c):
             bank = psum.tile([P, 2, 2, P], F32, name="back", tag="turn")
             for j in range(2):
                 for u in range(2):
                     nc.tensor.transpose(bank[:, j, u, :], pairs[:, j, u, :], ident[:])
-            woven = ring.tile([P, 2, P, 2], F32, name="woven", align_bytes=64)
-            move(out=woven[:], in_=bank[:].rearrange("p j u m -> p j m u"))
-            nc.vector.quantize_mx(
-                out=codes.bitcast(FP8X4), scales=scales, in_=woven[:].rearrange("p j m u -> p (j m u)").bitcast(BF16)
-            )
+            nc.scalar.copy(out=woven[:, c], in_=bank[:].rearrange("p j u m -> p j m u"))
 
-        def quantise_x(a):
-            for jj in range(2):
-                cols = slice(2 * jj * P, 2 * (jj + 1) * P)
-                turn_back(x_t[a][:, 2 * jj : 2 * jj + 2, :, :], x_w[a][:, cols], x_s[a][:, cols], nc.vector.tensor_copy if a == 1 else nc.scalar.copy)
+        def quantise(codes, scales, c, rounded):
+            cols = slice(c * CHUNK, c * CHUNK + rounded.shape[1] // PACK)
+            nc.vector.quantize_mx(out=codes[:, cols].bitcast(FP8X4), scales=scales[:, cols], in_=rounded)
 
-        def quantise_page(a, jj):
-            half, lo = divmod(2 * jj, 4)
-            words = page_t[a][half][:].rearrange("m j u p e -> m j u (p e)").bitcast(F32)
-            cols = slice(2 * jj * P, 2 * (jj + 1) * P)
-            turn_back(words[:, lo : lo + 2, :, :], page_w[a][:, cols], page_s[a][:, cols], nc.vector.tensor_copy if a == 1 and jj >= 2 else nc.scalar.copy)
+        def weave_page(i, c):
+            nc.scalar.copy(out=page_bf[c][:, :, i - PACK], in_=page[i][:, c * CHUNK : (c + 1) * CHUNK])
 
-        e_banks = {}
+        def weave_x(i):
+            cap_x(i, x_bf[:, :, i - PACK])
 
         def compare(j, passes):
             cols = slice(j * P, (j + 1) * P)
             if j not in e_banks:
-                e_banks[j] = psum.tile([P, NP], F32, name="e_bank", tag="sum")
+                tag, bufs = (("turn", 4), ("second", 2), ("first", 2))[max(0, j // 2 - 1)]
+                e_banks[j] = psum.tile([P, NP], F32, name="e_bank", tag=tag, bufs=bufs)
             bank = e_banks[j]
             for a in passes:
                 nc.tensor.matmul_mx(
@@ -275,47 +326,70 @@ def tile_list_guide_dog_pairing_kernel(
                 )
             if 1 not in passes:
                 return
-            dist = ring.tile([P, NP], F32, name="dist", bufs=4)
-            nc.scalar.activation(
-                out=dist[:], in_=bank[:], func=ACT.Abs, bias=rest_col[:, 2 * TILES + j : 2 * TILES + j + 1], scale=-1.0
-            )
+            dist = ring.tile([P, NP], F32, name="dist", bufs=6)
+            reference = rest_col[:, 2 * PACK + j : 2 * PACK + j + 1]
+            nc.scalar.activation(out=dist[:], in_=bank[:], func=ACT.Abs, bias=reference, scale=-1.0)
             nc.sync.dma_start(out=out[cols, :], in_=dist[:])
 
         spread(gain_rows, gain_col)
         for a in range(PASSES):
             nc.vector.tensor_copy(out=v_s[a][:], in_=tab_s[:, a * T : (a + 1) * T].indirect(pick[:]))
         nc.vector.tensor_copy(out=v_w[0][:], in_=tab_w[0][:].bitcast(U32).indirect(pick[:]))
+        round_w1(0)
         quantise_w1(0)
         nc.vector.tensor_copy(out=v_w[1][:], in_=tab_w[1][:].bitcast(U32).indirect(pick[:]))
         read_table(0)
+        round_w1(1)
         quantise_w1(1)
-        combine(0)
-        spread(rest_rows, rest_col)
         read_table(1)
+        combine(0)
+        round_w1(2)
+        quantise_w1(2)
+        read_table(2)
+        spread(rest_rows, rest_col)
+        round_w1(3)
+        spread(dealt_rows, dealt_col)
+        last = TILES - 1
+        combine(1)
         for i in range(TILES):
-            if i + 2 < TILES:
-                quantise_w1(i + 2)
-            if i + 1 < TILES:
-                combine(i + 1)
-            if i + 2 < TILES:
-                read_table(i + 2)
             scatter(i)
-            if i > 0:
-                turn_x(i - 1)
             gather(i)
-            turn_page(i)
-            if i == 4:
-                quantise_x(0)
-            if 4 <= i < 6:
-                quantise_page(0, 2 * (i - 4))
-                quantise_page(0, 2 * (i - 4) + 1)
-        for j in range(4):
-            compare(j, [0])
-        turn_x(TILES - 1)
-        quantise_page(1, 0)
-        quantise_x(1)
-        for jj in range(4):
-            if jj + 1 < 4:
-                quantise_page(1, jj + 1)
-            for j in (2 * jj, 2 * jj + 1):
-                compare(j, [1] if j < 4 else [0, 1])
+            if i + 4 < TILES:
+                round_w1(i + 4)
+            if i == 1:
+                deal_w2()
+            if i + 3 < TILES:
+                quantise_w1(i + 3)
+            if i == 5:
+                x_w[0] = reuse.tile([P, NP], U32, name="x_w0", align_bytes=64, offset=weighted_at[5] - ROW // 2)
+                page_w[0] = reuse.tile([P, T2], U32, name="page_w0", align_bytes=64, offset=weighted_at[5] + ROW // 2)
+                quantise(page_w[0], page_s[0], 0, woven[:, 2:].rearrange("p c j m u -> p (c j m u)").bitcast(BF16))
+                quantise(x_w[0], x_s[0], 0, woven[:, :2].rearrange("p c j m u -> p (c j m u)").bitcast(BF16))
+            if i < PACK:
+                turn_x(i)
+            else:
+                weave_x(i)
+            if i + 2 < TILES:
+                combine(i + 2)
+            if i + 3 < TILES:
+                read_table(i + 3)
+            if i < PACK:
+                turn_page(i)
+            elif i < last:
+                for c in range(T2 // CHUNK):
+                    weave_page(i, c)
+            if i == PACK - 1:
+                for c in range(4):
+                    words = page_t[c // 2][:].rearrange("m j u p e -> m j u (p e)").bitcast(F32)
+                    turn_back(words[:, 2 * (c % 2) : 2 * (c % 2) + 2, :, :], 2 + c)
+                for c in range(2):
+                    turn_back(x_t[:, 2 * c : 2 * c + 2, :, :], c)
+            if i == last - 1:
+                for j in range(TILES):
+                    compare(j, [0])
+        quantise(x_w[1], x_s[1], 0, x_bf[:].rearrange("p n t -> p (n t)"))
+        for c in range(T2 // CHUNK):
+            weave_page(last, c)
+            quantise(page_w[1], page_s[1], c, page_bf[c][:].rearrange("p m t -> p (m t)"))
+        for j in range(TILES):
+            compare(j, [1])

@@ -10,8 +10,12 @@ K_PASS = P * PACK
 PASSES = 2
 TILES = H // P
 QUAD = 32
+QUADS = P // QUAD
+BLOCKS = NP // P
 CHUNK = 256
 RUN = 8
+AHEAD = 3
+LATE = 5
 FLOPS = 2 * (2 * K * H * S + H * T2 * NP)
 
 F32 = mybir.dt.float32
@@ -62,10 +66,14 @@ def tile_list_guide_dog_pairing_kernel(
         rest_col = keep.tile([P, 2 * PACK + TILES], F32, name="rest_col")
         dealt_rows = keep.tile([P, P], F32, name="dealt_rows")
         dealt_col = keep.tile([P, 3 * PACK], F32, name="dealt_col")
-        page_t = [reuse.tile([P, 4, 2, P, 2], BF16, name=f"page_t{h}", offset=(18 + 2 * h) * ROW) for h in range(2)]
-        x_t = reuse.tile([P, 4, 2, P], F32, name="x_t", offset=22 * ROW)
+        turned_at = 18 * ROW
+        page_t = [
+            reuse.tile([P, BLOCKS, 2, P, 2], BF16, name=f"page_t{half}", offset=turned_at + 2 * half * ROW)
+            for half in range(2)
+        ]
+        x_t = reuse.tile([P, BLOCKS, 2, P], F32, name="x_t", offset=turned_at + 4 * ROW)
         page_bf = [
-            reuse.tile([P, CHUNK, PACK], BF16, name=f"page_bf{c}", align_bytes=64, offset=(23 - c) * ROW)
+            reuse.tile([P, CHUNK, PACK], BF16, name=f"page_bf{c}", align_bytes=64, offset=turned_at + (5 - c) * ROW)
             for c in range(T2 // CHUNK)
         ]
         x_bf = keep.tile([P, NP, PACK], BF16, name="x_bf", align_bytes=64)
@@ -73,19 +81,18 @@ def tile_list_guide_dog_pairing_kernel(
         x_s = [keep.tile([P, NP], U8, name=f"x_s{a}", align_bytes=64) for a in range(PASSES)]
 
         w1_bf = [keep.tile([P, PASSES, P, PACK], BF16, name=f"w1_bf{i}", align_bytes=64) for i in range(TILES)]
-        weighted_at = [i * ROW for i in range(5)] + [6 * ROW, 9 * ROW, 10 * ROW]
-        codes_at = [11 * ROW + i * ROW // 2 for i in range(3)] + weighted_at[:5]
+        weighted_at = [i * ROW for i in range(LATE)] + [(LATE + 1) * ROW, (LATE + 4) * ROW, (LATE + 5) * ROW]
+        codes_at = [11 * ROW + i * ROW // 2 for i in range(AHEAD)] + weighted_at[: TILES - AHEAD]
         picked_at = [(13 + 2 * (i % 2)) * ROW for i in range(TILES)]
-        woven = keep.tile([P, 6, 2, P, 2], F32, name="woven", align_bytes=64)
+        x_chunks, page_chunks = NP // CHUNK, T2 // CHUNK
+        woven = keep.tile([P, x_chunks + page_chunks, 2, P, 2], F32, name="woven", align_bytes=64)
         x_w = [None, keep.tile([P, NP], U32, name="x_w1", align_bytes=64)]
         page_w = [None, keep.tile([P, T2], U32, name="page_w1", align_bytes=64)]
 
         def load_scales(plane, scales):
             rows = scales.bitcast(I32)
-            for q in range(4):
-                nc.sync.dma_start(
-                    out=plane[QUAD * q : QUAD * q + 4], in_=rows[:, 4 * q : 4 * q + 4, :].rearrange("a r c -> r a c")
-                )
+            for r in range(4):
+                nc.sync.dma_start(out=plane[r:P:QUAD], in_=rows[:, r::4, :].rearrange("a q c -> q a c"))
 
         def load_table(a):
             nc.sync.dma_start(out=tab_w[a][:], in_=tab_words[a].rearrange("p t i -> p (t i)").bitcast(I32))
@@ -104,7 +111,7 @@ def tile_list_guide_dog_pairing_kernel(
             if i < PACK:
                 rows = page0[i * P : (i + 1) * P, :]
             else:
-                rows = page0[K_PASS:, :].rearrange("(g t i) m -> t g i m", t=PACK, i=RUN)[i - PACK]
+                rows = page0[K_PASS:, :].rearrange("(g t n) m -> t g n m", t=PACK, n=RUN)[i - PACK]
             nc.sync.dma_start(out=page[i][:], in_=rows)
 
         nc.gpsimd.memset(tab_s[:].bitcast(I32), 0)
@@ -113,7 +120,7 @@ def tile_list_guide_dog_pairing_kernel(
         nc.vector.memset(rest_rows[:], 0.0)
         nc.vector.memset(dealt_rows[:], 0.0)
         make_identity(nc, ident[:])
-        nc.vector.tensor_copy(out=ident_bf[:], in_=ident[:])
+        nc.scalar.activation(out=ident_bf[:], in_=ident[:], func=ACT.Identity)
 
         nc.sync.dma_start(pick[:], offs)
         load_table(0)
@@ -141,7 +148,7 @@ def tile_list_guide_dog_pairing_kernel(
         load_page(2)
         load_page(3)
         for t in range(PACK):
-            for q in range(4):
+            for q in range(QUADS):
                 rows = wgs.rearrange("(g t i) j -> t g i j", t=PACK, i=RUN)[t]
                 nc.sync.dma_start(out=wg_dealt[QUAD * q : QUAD * (q + 1), t, :], in_=rows)
             load_page(PACK + t)
@@ -170,13 +177,13 @@ def tile_list_guide_dog_pairing_kernel(
                 blk = min(i, 2)
                 c0 = i * P - w1_blocks[blk][0]
                 nc.scalar.copy(
-                    out=w1_bf[i][:].rearrange("p a (c i) j -> p a c j i", i=4),
-                    in_=w1_raw[blk][:, :, :, c0 : c0 + P].rearrange("p a j (c i) -> p a c j i", i=4),
+                    out=w1_bf[i][:].rearrange("p a (c n) j -> p a c j n", n=PACK),
+                    in_=w1_raw[blk][:, :, :, c0 : c0 + P].rearrange("p a j (c n) -> p a c j n", n=PACK),
                 )
             else:
                 nc.scalar.copy(
-                    out=w1_bf[i][:].rearrange("p a (g i) j -> p a g j i", i=RUN),
-                    in_=w1_raw[3][:].rearrange("p a j (g t i) -> p t a g j i", t=PACK, i=RUN)[:, i - PACK],
+                    out=w1_bf[i][:].rearrange("p a (g n) j -> p a g j n", n=RUN),
+                    in_=w1_raw[-1][:].rearrange("p a j (g t n) -> p t a g j n", t=PACK, n=RUN)[:, i - PACK],
                 )
 
         def deal_w2():
@@ -190,11 +197,10 @@ def tile_list_guide_dog_pairing_kernel(
             )
 
         def quantise_w1(i):
-            rounded = w1_bf[i][:]
             codes = reuse.tile([P, PASSES * P], U32, name=f"w1_w{i}", align_bytes=64, offset=codes_at[i])
             scales = ring.tile([P, PASSES * P], U8, name="w1_s", align_bytes=64)
             nc.vector.quantize_mx(
-                out=codes[:].bitcast(FP8X4), scales=scales[:], in_=rounded.rearrange("p a c j -> p (a c j)")
+                out=codes[:].bitcast(FP8X4), scales=scales[:], in_=w1_bf[i][:].rearrange("p a c j -> p (a c j)")
             )
             w1_q[i] = (codes, scales)
 
@@ -271,9 +277,9 @@ def tile_list_guide_dog_pairing_kernel(
 
         def turn_page(i):
             for half in range(2):
-                bank = psum.tile([P, 4, P], F32, name="page_turn", tag="turn")
-                for j in range(4):
-                    m0 = (4 * half + j) * P
+                bank = psum.tile([P, BLOCKS, P], F32, name="page_turn", tag="turn")
+                for j in range(BLOCKS):
+                    m0 = (BLOCKS * half + j) * P
                     nc.tensor.transpose(bank[:, j, :], page[i][:, m0 : m0 + P], ident[:])
                 nc.scalar.copy(
                     out=page_t[half][:, :, :, QUAD * i : QUAD * (i + 1), :],
@@ -283,8 +289,8 @@ def tile_list_guide_dog_pairing_kernel(
         def turn_x(i):
             x = ring.tile([P, NP], BF16, name="x", bufs=2)
             cap_x(i, x[:])
-            bank = psum.tile([P, 4, P], BF16, name="x_turn", tag="turn")
-            for j in range(4):
+            bank = psum.tile([P, BLOCKS, P], BF16, name="x_turn", tag="turn")
+            for j in range(BLOCKS):
                 nc.tensor.transpose(bank[:, j, :], x[:, j * P : (j + 1) * P], ident_bf[:])
             nc.scalar.copy(
                 out=x_t[:, :, :, QUAD * i : QUAD * (i + 1)],
@@ -305,31 +311,23 @@ def tile_list_guide_dog_pairing_kernel(
         def weave_page(i, c):
             nc.scalar.copy(out=page_bf[c][:, :, i - PACK], in_=page[i][:, c * CHUNK : (c + 1) * CHUNK])
 
-        def weave_x(i):
-            cap_x(i, x_bf[:, :, i - PACK])
-
-        def compare(j, passes):
+        def compare(j, a):
             cols = slice(j * P, (j + 1) * P)
-            if j not in e_banks:
-                tag, bufs = (("turn", 4), ("second", 2), ("first", 2))[max(0, j // 2 - 1)]
-                e_banks[j] = psum.tile([P, NP], F32, name="e_bank", tag=tag, bufs=bufs)
-            bank = e_banks[j]
-            for a in passes:
-                nc.tensor.matmul_mx(
-                    out=bank[:],
-                    lhsT=page_w[a][:, cols].bitcast(FP8X4),
-                    lhsT_scale=page_s[a][:, cols],
-                    rhs=x_w[a][:].bitcast(FP8X4),
-                    rhs_scale=x_s[a][:],
-                    start=(a == 0),
-                    stop=(a == PASSES - 1),
-                )
-            if 1 not in passes:
-                return
+            nc.tensor.matmul_mx(
+                out=e_banks[j][:],
+                lhsT=page_w[a][:, cols].bitcast(FP8X4),
+                lhsT_scale=page_s[a][:, cols],
+                rhs=x_w[a][:].bitcast(FP8X4),
+                rhs_scale=x_s[a][:],
+                start=(a == 0),
+                stop=(a == PASSES - 1),
+            )
+
+        def store(j):
             dist = ring.tile([P, NP], F32, name="dist", bufs=6)
             reference = rest_col[:, 2 * PACK + j : 2 * PACK + j + 1]
-            nc.scalar.activation(out=dist[:], in_=bank[:], func=ACT.Abs, bias=reference, scale=-1.0)
-            nc.sync.dma_start(out=out[cols, :], in_=dist[:])
+            nc.scalar.activation(out=dist[:], in_=e_banks[j][:], func=ACT.Abs, bias=reference, scale=-1.0)
+            nc.sync.dma_start(out=out[j * P : (j + 1) * P, :], in_=dist[:])
 
         spread(gain_rows, gain_col)
         for a in range(PASSES):
@@ -349,47 +347,55 @@ def tile_list_guide_dog_pairing_kernel(
         spread(rest_rows, rest_col)
         round_w1(3)
         spread(dealt_rows, dealt_col)
-        last = TILES - 1
         combine(1)
+
+        last = TILES - 1
         for i in range(TILES):
             scatter(i)
             gather(i)
-            if i + 4 < TILES:
-                round_w1(i + 4)
-            if i == 1:
+            if i + AHEAD + 1 < TILES:
+                round_w1(i + AHEAD + 1)
+            if i + AHEAD == PACK:
                 deal_w2()
-            if i + 3 < TILES:
-                quantise_w1(i + 3)
-            if i == 5:
-                x_w[0] = reuse.tile([P, NP], U32, name="x_w0", align_bytes=64, offset=weighted_at[5] - ROW // 2)
-                page_w[0] = reuse.tile([P, T2], U32, name="page_w0", align_bytes=64, offset=weighted_at[5] + ROW // 2)
-                quantise(page_w[0], page_s[0], 0, woven[:, 2:].rearrange("p c j m u -> p (c j m u)").bitcast(BF16))
-                quantise(x_w[0], x_s[0], 0, woven[:, :2].rearrange("p c j m u -> p (c j m u)").bitcast(BF16))
+            if i + AHEAD < TILES:
+                quantise_w1(i + AHEAD)
+            if i == LATE:
+                x_w[0] = reuse.tile([P, NP], U32, name="x_w0", align_bytes=64, offset=weighted_at[LATE] - ROW // 2)
+                page_w[0] = reuse.tile([P, T2], U32, name="page_w0", align_bytes=64, offset=weighted_at[LATE] + ROW // 2)
+                for codes, scales, words in (
+                    (page_w[0], page_s[0], woven[:, x_chunks:]),
+                    (x_w[0], x_s[0], woven[:, :x_chunks]),
+                ):
+                    quantise(codes, scales, 0, words.rearrange("p c j m u -> p (c j m u)").bitcast(BF16))
             if i < PACK:
                 turn_x(i)
             else:
-                weave_x(i)
+                cap_x(i, x_bf[:, :, i - PACK])
             if i + 2 < TILES:
                 combine(i + 2)
-            if i + 3 < TILES:
-                read_table(i + 3)
+            if i + AHEAD < TILES:
+                read_table(i + AHEAD)
             if i < PACK:
                 turn_page(i)
             elif i < last:
-                for c in range(T2 // CHUNK):
+                for c in range(page_chunks):
                     weave_page(i, c)
             if i == PACK - 1:
-                for c in range(4):
+                for c in range(page_chunks):
                     words = page_t[c // 2][:].rearrange("m j u p e -> m j u (p e)").bitcast(F32)
-                    turn_back(words[:, 2 * (c % 2) : 2 * (c % 2) + 2, :, :], 2 + c)
-                for c in range(2):
+                    turn_back(words[:, 2 * (c % 2) : 2 * (c % 2) + 2, :, :], x_chunks + c)
+                for c in range(x_chunks):
                     turn_back(x_t[:, 2 * c : 2 * c + 2, :, :], c)
             if i == last - 1:
-                for j in range(TILES):
-                    compare(j, [0])
+                banks = [("turn", 4)] * 4 + [("second", 2)] * 2 + [("first", 2)] * 2
+                for j, (tag, bufs) in enumerate(banks):
+                    e_banks[j] = psum.tile([P, NP], F32, name="e_bank", tag=tag, bufs=bufs)
+                    compare(j, 0)
+
         quantise(x_w[1], x_s[1], 0, x_bf[:].rearrange("p n t -> p (n t)"))
-        for c in range(T2 // CHUNK):
+        for c in range(page_chunks):
             weave_page(last, c)
             quantise(page_w[1], page_s[1], c, page_bf[c][:].rearrange("p m t -> p (m t)"))
         for j in range(TILES):
-            compare(j, [1])
+            compare(j, 1)
+            store(j)

from contextlib import ExitStack

import concourse.mybir as mybir
from concourse.masks import make_identity

K, T, S, H, T2, NP = 1024, 2048, 512, 1024, 1024, 512
P = 128
PACK = 4
K_PASS = P * PACK
PASSES = 2
TILES = H // P
QUAD = 32
QUADS = P // QUAD
BLOCKS = NP // P
CHUNK = 256
RUN = 8
AHEAD = 3
LATE = 5
FLOPS = 2 * (2 * K * H * S + H * T2 * NP)

F32 = mybir.dt.float32
BF16 = mybir.dt.bfloat16
I32 = mybir.dt.int32
U32 = mybir.dt.uint32
U16 = mybir.dt.uint16
U8 = mybir.dt.uint8
FP8X4 = mybir.dt.float8_e4m3fn_x4
FP4X4 = mybir.dt.float4_e2m1fn_x4
ALU = mybir.AluOpType
ACT = mybir.ActivationFunctionType

ROW = 4 * S


def tile_list_guide_dog_pairing_kernel(
    tc, tab_words, tab_scales, offs, w1, w2_words, w2_scales, gain, wgs, page0, offs2, offs3, cap, vec, slot, out
):
    nc = tc.nc
    with ExitStack() as ctx:
        keep = ctx.enter_context(tc.tile_pool(name="keep", bufs=1))
        reuse = ctx.enter_context(tc.tile_pool(name="reuse", bufs=1))
        ring = ctx.enter_context(tc.tile_pool(name="ring", bufs=4))
        psum = ctx.enter_context(tc.psum_pool(name="psum", bufs=4))

        pick = keep.tile([P, S // 16], U16, name="pick")
        place = keep.tile([P, S // 16], U16, name="place")
        cand = keep.tile([P, NP // 16], U16, name="cand")
        tab_w = [keep.tile([P, T], I32, name=f"tab_w{a}") for a in range(PASSES)]
        tab_s = keep.tile([P, PASSES * T], U8, name="tab_s")
        v_w = [keep.tile([P, S], U32, name=f"v_w{a}", align_bytes=64) for a in range(PASSES)]
        v_s = [keep.tile([P, S], U8, name=f"v_s{a}", align_bytes=64) for a in range(PASSES)]
        w1_blocks = [(0, P), (P, P), (2 * P, 2 * P), (K_PASS, K_PASS)]
        w1_raw = [keep.tile([P, PASSES, PACK, n], F32, name=f"w1_raw{c0}") for c0, n in w1_blocks]
        w2_w = [keep.tile([P, PASSES, K_PASS // 2], I32, name=f"w2_w{n}", align_bytes=64) for n in range(2)]
        w2_s = keep.tile([P, PASSES, H // 4], I32, name="w2_s", align_bytes=64)
        w2_w_dealt = keep.tile([P, PASSES, PACK, P // 2], I32, name="w2_w_dealt", align_bytes=64)
        w2_s_dealt = keep.tile([P, PASSES, PACK, P // 4], I32, name="w2_s_dealt", align_bytes=64)
        page = [keep.tile([P, T2], F32, name=f"page{i}") for i in range(TILES)]
        wg = keep.tile([P, S], F32, name="wg")
        wg_dealt = keep.tile([P, PACK, S], F32, name="wg_dealt")
        ident = keep.tile([P, P], F32, name="ident")
        ident_bf = keep.tile([P, P], BF16, name="ident_bf")
        gain_rows = keep.tile([P, P], F32, name="gain_rows")
        rest_rows = keep.tile([P, P], F32, name="rest_rows")
        gain_col = keep.tile([P, PACK], F32, name="gain_col")
        rest_col = keep.tile([P, 2 * PACK + TILES], F32, name="rest_col")
        dealt_rows = keep.tile([P, P], F32, name="dealt_rows")
        dealt_col = keep.tile([P, 3 * PACK], F32, name="dealt_col")
        turned_at = 18 * ROW
        page_t = [
            reuse.tile([P, BLOCKS, 2, P, 2], BF16, name=f"page_t{half}", offset=turned_at + 2 * half * ROW)
            for half in range(2)
        ]
        x_t = reuse.tile([P, BLOCKS, 2, P], F32, name="x_t", offset=turned_at + 4 * ROW)
        page_bf = [
            reuse.tile([P, CHUNK, PACK], BF16, name=f"page_bf{c}", align_bytes=64, offset=turned_at + (5 - c) * ROW)
            for c in range(T2 // CHUNK)
        ]
        x_bf = keep.tile([P, NP, PACK], BF16, name="x_bf", align_bytes=64)
        page_s = [keep.tile([P, T2], U8, name=f"page_s{a}", align_bytes=64) for a in range(PASSES)]
        x_s = [keep.tile([P, NP], U8, name=f"x_s{a}", align_bytes=64) for a in range(PASSES)]

        w1_bf = [keep.tile([P, PASSES, P, PACK], BF16, name=f"w1_bf{i}", align_bytes=64) for i in range(TILES)]
        weighted_at = [i * ROW for i in range(LATE)] + [(LATE + 1) * ROW, (LATE + 4) * ROW, (LATE + 5) * ROW]
        codes_at = [11 * ROW + i * ROW // 2 for i in range(AHEAD)] + weighted_at[: TILES - AHEAD]
        picked_at = [(13 + 2 * (i % 2)) * ROW for i in range(TILES)]
        x_chunks, page_chunks = NP // CHUNK, T2 // CHUNK
        woven = keep.tile([P, x_chunks + page_chunks, 2, P, 2], F32, name="woven", align_bytes=64)
        x_w = [None, keep.tile([P, NP], U32, name="x_w1", align_bytes=64)]
        page_w = [None, keep.tile([P, T2], U32, name="page_w1", align_bytes=64)]

        def load_scales(plane, scales):
            rows = scales.bitcast(I32)
            for r in range(4):
                nc.sync.dma_start(out=plane[r:P:QUAD], in_=rows[:, r::4, :].rearrange("a q c -> q a c"))

        def load_table(a):
            nc.sync.dma_start(out=tab_w[a][:], in_=tab_words[a].rearrange("p t i -> p (t i)").bitcast(I32))

        def load_w1(blk):
            c0, n = w1_blocks[blk]
            for a in range(PASSES):
                rows = w1[a * K_PASS : (a + 1) * K_PASS, c0 : c0 + n]
                nc.sync.dma_start(out=w1_raw[blk][:, a, :, :], in_=rows.rearrange("(p j) c -> p j c", j=PACK))

        def load_w2(n):
            words = w2_words.bitcast(I32).rearrange("a p (n c) -> n p a c", n=2)
            nc.sync.dma_start(out=w2_w[n][:], in_=words[n])

        def load_page(i):
            if i < PACK:
                rows = page0[i * P : (i + 1) * P, :]
            else:
                rows = page0[K_PASS:, :].rearrange("(g t n) m -> t g n m", t=PACK, n=RUN)[i - PACK]
            nc.sync.dma_start(out=page[i][:], in_=rows)

        nc.gpsimd.memset(tab_s[:].bitcast(I32), 0)
        nc.vector.memset(w2_s[:], 0)
        nc.vector.memset(gain_rows[:], 0.0)
        nc.vector.memset(rest_rows[:], 0.0)
        nc.vector.memset(dealt_rows[:], 0.0)
        make_identity(nc, ident[:])
        nc.scalar.activation(out=ident_bf[:], in_=ident[:], func=ACT.Identity)

        nc.sync.dma_start(pick[:], offs)
        load_table(0)
        load_scales(tab_s[:].bitcast(I32).rearrange("p (a c) -> p a c", a=PASSES), tab_scales)
        load_w1(0)
        load_table(1)
        load_scales(w2_s[:], w2_scales)
        load_w2(0)
        nc.sync.dma_start(out=gain_rows[0:PACK, :], in_=gain[:K_PASS].rearrange("(i p) -> i p", p=P))
        load_w1(1)
        load_page(0)
        nc.sync.dma_start(place[:], offs2)
        nc.sync.dma_start(out=wg[:], in_=wgs)
        load_w1(2)
        nc.sync.dma_start(cand[:], offs3)
        for n, v in enumerate((cap[:K_PASS], vec[:K_PASS], slot)):
            rows = v.rearrange("(i p) -> i p", p=P)
            nc.sync.dma_start(out=rest_rows[n * PACK : n * PACK + rows.shape[0], :], in_=rows)
        load_w1(3)
        load_page(1)
        load_w2(1)
        for n, v in enumerate((gain, cap, vec)):
            rows = v[K_PASS:].rearrange("(g t i) -> t g i", t=PACK, i=RUN)
            nc.sync.dma_start(out=dealt_rows[n * PACK : (n + 1) * PACK, :].rearrange("t (g i) -> t g i", i=RUN), in_=rows)
        load_page(2)
        load_page(3)
        for t in range(PACK):
            for q in range(QUADS):
                rows = wgs.rearrange("(g t i) j -> t g i j", t=PACK, i=RUN)[t]
                nc.sync.dma_start(out=wg_dealt[QUAD * q : QUAD * (q + 1), t, :], in_=rows)
            load_page(PACK + t)

        def spread(rows, cols):
            bank = psum.tile([P, P], F32, name="spread", tag="turn")
            nc.tensor.transpose(bank[:], rows[:], ident[:])
            nc.scalar.copy(out=cols[:], in_=bank[:, 0 : cols.shape[1]])

        def column(n, i):
            if i >= PACK:
                c = (n - 1) * PACK + i
                return dealt_col[:, c : c + 1]
            if n == 0:
                return gain_col[:, i : i + 1]
            return rest_col[:, (n - 1) * PACK + i : (n - 1) * PACK + i + 1]

        w1_q = {}
        readings = {}
        revised = {}
        picked = {}
        e_banks = {}

        def round_w1(i):
            if i < PACK:
                blk = min(i, 2)
                c0 = i * P - w1_blocks[blk][0]
                nc.scalar.copy(
                    out=w1_bf[i][:].rearrange("p a (c n) j -> p a c j n", n=PACK),
                    in_=w1_raw[blk][:, :, :, c0 : c0 + P].rearrange("p a j (c n) -> p a c j n", n=PACK),
                )
            else:
                nc.scalar.copy(
                    out=w1_bf[i][:].rearrange("p a (g n) j -> p a g j n", n=RUN),
                    in_=w1_raw[-1][:].rearrange("p a j (g t n) -> p t a g j n", t=PACK, n=RUN)[:, i - PACK],
                )

        def deal_w2():
            nc.vector.tensor_copy(
                out=w2_w_dealt[:].rearrange("p a t (g w) -> p a t g w", w=RUN // 2),
                in_=w2_w[1][:].rearrange("p a (g t w) -> p a t g w", t=PACK, w=RUN // 2),
            )
            nc.vector.tensor_copy(
                out=w2_s_dealt[:].rearrange("p a t (g w) -> p a t g w", w=RUN // 4),
                in_=w2_s[:, :, K_PASS // 4 :].rearrange("p a (g t w) -> p a t g w", t=PACK, w=RUN // 4),
            )

        def quantise_w1(i):
            codes = reuse.tile([P, PASSES * P], U32, name=f"w1_w{i}", align_bytes=64, offset=codes_at[i])
            scales = ring.tile([P, PASSES * P], U8, name="w1_s", align_bytes=64)
            nc.vector.quantize_mx(
                out=codes[:].bitcast(FP8X4), scales=scales[:], in_=w1_bf[i][:].rearrange("p a c j -> p (a c j)")
            )
            w1_q[i] = (codes, scales)

        def read_table(i):
            codes, scales = w1_q[i]
            a_bank = psum.tile([P, S], F32, name="a_bank", tag="first", bufs=2)
            b_bank = psum.tile([P, S], F32, name="b_bank", tag="second", bufs=2)
            for a in range(PASSES):
                if i < PACK:
                    words, plane = w2_w[0][:, a, i * P // 2 : (i + 1) * P // 2], w2_s[:, a, i * P // 4 : (i + 1) * P // 4]
                else:
                    words, plane = w2_w_dealt[:, a, i - PACK], w2_s_dealt[:, a, i - PACK]
                nc.tensor.matmul_mx(
                    out=b_bank[:],
                    lhsT=words.bitcast(FP4X4),
                    lhsT_scale=plane.bitcast(U8),
                    rhs=v_w[a][:].bitcast(FP8X4),
                    rhs_scale=v_s[a][:],
                    start=(a == 0),
                    stop=(a == PASSES - 1),
                )
            for a in range(PASSES):
                nc.tensor.matmul_mx(
                    out=a_bank[:],
                    lhsT=codes[:, a * P : (a + 1) * P].bitcast(FP8X4),
                    lhsT_scale=scales[:, a * P : (a + 1) * P],
                    rhs=v_w[a][:].bitcast(FP8X4),
                    rhs_scale=v_s[a][:],
                    start=(a == 0),
                    stop=(a == PASSES - 1),
                )
            b_sb = ring.tile([P, S], F32, name="b_sb", bufs=3)
            nc.scalar.copy(out=b_sb[:], in_=b_bank[:])
            if i == 0:
                readings[i] = (a_bank, b_sb)
                return
            b_gain = ring.tile([P, S], F32, name="b_gain", bufs=3)
            nc.scalar.activation(out=b_gain[:], in_=b_bank[:], func=ACT.Identity, bias=column(0, i))
            a_sb = ring.tile([P, S], F32, name="a_sb", bufs=3)
            nc.scalar.copy(out=a_sb[:], in_=a_bank[:])
            readings[i] = (a_sb, b_sb, b_gain)

        def weights(i):
            return wg[:] if i < PACK else wg_dealt[:, i - PACK]

        def combine(i):
            prod = reuse.tile([P, S], F32, name=f"prod{i}", offset=picked_at[i] + ROW // 2)
            h = reuse.tile([P, S], F32, name=f"h{i}", offset=picked_at[i - 1] + ROW)
            revised[i] = reuse.tile([P, S], F32, name=f"weighted{i}", offset=weighted_at[i])[:]
            if i == 0:
                a_bank, b_sb = readings[i]
                nc.vector.scalar_tensor_tensor(
                    out=prod[:], in0=b_sb[:], scalar=column(0, i), in1=a_bank[:], op0=ALU.add, op1=ALU.mult
                )
                nc.vector.tensor_tensor(out=h[:], in0=prod[:], in1=b_sb[:], op=ALU.add)
                nc.vector.tensor_tensor(out=revised[i], in0=h[:], in1=weights(i), op=ALU.mult)
                return
            a_sb, b_sb, b_gain = readings[i]
            nc.gpsimd.tensor_tensor(out=prod[:], in0=a_sb[:], in1=b_gain[:], op=ALU.mult)
            nc.gpsimd.tensor_tensor(out=h[:], in0=prod[:], in1=b_sb[:], op=ALU.add)
            nc.gpsimd.tensor_tensor(out=revised[i], in0=h[:], in1=weights(i), op=ALU.mult)

        def scatter(i):
            nc.vector.tensor_copy(out=page[i][:].indirect(place[:]), in_=revised[i])

        def gather(i):
            picked[i] = reuse.tile([P, NP], F32, name=f"picked{i}", offset=picked_at[i])[:]
            nc.vector.tensor_copy(out=picked[i], in_=page[i][:].indirect(cand[:]))

        def cap_x(i, x):
            nc.vector.tensor_scalar(
                out=x, in0=picked[i], scalar1=column(1, i), scalar2=column(2, i), op0=ALU.min, op1=ALU.mult
            )

        def turn_page(i):
            for half in range(2):
                bank = psum.tile([P, BLOCKS, P], F32, name="page_turn", tag="turn")
                for j in range(BLOCKS):
                    m0 = (BLOCKS * half + j) * P
                    nc.tensor.transpose(bank[:, j, :], page[i][:, m0 : m0 + P], ident[:])
                nc.scalar.copy(
                    out=page_t[half][:, :, :, QUAD * i : QUAD * (i + 1), :],
                    in_=bank[:].rearrange("m j (p u e) -> m j u p e", u=2, e=2),
                )

        def turn_x(i):
            x = ring.tile([P, NP], BF16, name="x", bufs=2)
            cap_x(i, x[:])
            bank = psum.tile([P, BLOCKS, P], BF16, name="x_turn", tag="turn")
            for j in range(BLOCKS):
                nc.tensor.transpose(bank[:, j, :], x[:, j * P : (j + 1) * P], ident_bf[:])
            nc.scalar.copy(
                out=x_t[:, :, :, QUAD * i : QUAD * (i + 1)],
                in_=bank[:].bitcast(F32).rearrange("n j (p u) -> n j u p", u=2),
            )

        def turn_back(pairs, c):
            bank = psum.tile([P, 2, 2, P], F32, name="back", tag="turn")
            for j in range(2):
                for u in range(2):
                    nc.tensor.transpose(bank[:, j, u, :], pairs[:, j, u, :], ident[:])
            nc.scalar.copy(out=woven[:, c], in_=bank[:].rearrange("p j u m -> p j m u"))

        def quantise(codes, scales, c, rounded):
            cols = slice(c * CHUNK, c * CHUNK + rounded.shape[1] // PACK)
            nc.vector.quantize_mx(out=codes[:, cols].bitcast(FP8X4), scales=scales[:, cols], in_=rounded)

        def weave_page(i, c):
            nc.scalar.copy(out=page_bf[c][:, :, i - PACK], in_=page[i][:, c * CHUNK : (c + 1) * CHUNK])

        def compare(j, a):
            cols = slice(j * P, (j + 1) * P)
            nc.tensor.matmul_mx(
                out=e_banks[j][:],
                lhsT=page_w[a][:, cols].bitcast(FP8X4),
                lhsT_scale=page_s[a][:, cols],
                rhs=x_w[a][:].bitcast(FP8X4),
                rhs_scale=x_s[a][:],
                start=(a == 0),
                stop=(a == PASSES - 1),
            )

        def store(j):
            dist = ring.tile([P, NP], F32, name="dist", bufs=6)
            reference = rest_col[:, 2 * PACK + j : 2 * PACK + j + 1]
            nc.scalar.activation(out=dist[:], in_=e_banks[j][:], func=ACT.Abs, bias=reference, scale=-1.0)
            nc.sync.dma_start(out=out[j * P : (j + 1) * P, :], in_=dist[:])

        spread(gain_rows, gain_col)
        for a in range(PASSES):
            nc.vector.tensor_copy(out=v_s[a][:], in_=tab_s[:, a * T : (a + 1) * T].indirect(pick[:]))
        nc.vector.tensor_copy(out=v_w[0][:], in_=tab_w[0][:].bitcast(U32).indirect(pick[:]))
        round_w1(0)
        quantise_w1(0)
        nc.vector.tensor_copy(out=v_w[1][:], in_=tab_w[1][:].bitcast(U32).indirect(pick[:]))
        read_table(0)
        round_w1(1)
        quantise_w1(1)
        read_table(1)
        combine(0)
        round_w1(2)
        quantise_w1(2)
        read_table(2)
        spread(rest_rows, rest_col)
        round_w1(3)
        spread(dealt_rows, dealt_col)
        combine(1)

        last = TILES - 1
        for i in range(TILES):
            scatter(i)
            gather(i)
            if i + AHEAD + 1 < TILES:
                round_w1(i + AHEAD + 1)
            if i + AHEAD == PACK:
                deal_w2()
            if i + AHEAD < TILES:
                quantise_w1(i + AHEAD)
            if i == LATE:
                x_w[0] = reuse.tile([P, NP], U32, name="x_w0", align_bytes=64, offset=weighted_at[LATE] - ROW // 2)
                page_w[0] = reuse.tile([P, T2], U32, name="page_w0", align_bytes=64, offset=weighted_at[LATE] + ROW // 2)
                for codes, scales, words in (
                    (page_w[0], page_s[0], woven[:, x_chunks:]),
                    (x_w[0], x_s[0], woven[:, :x_chunks]),
                ):
                    quantise(codes, scales, 0, words.rearrange("p c j m u -> p (c j m u)").bitcast(BF16))
            if i < PACK:
                turn_x(i)
            else:
                cap_x(i, x_bf[:, :, i - PACK])
            if i + 2 < TILES:
                combine(i + 2)
            if i + AHEAD < TILES:
                read_table(i + AHEAD)
            if i < PACK:
                turn_page(i)
            elif i < last:
                for c in range(page_chunks):
                    weave_page(i, c)
            if i == PACK - 1:
                for c in range(page_chunks):
                    words = page_t[c // 2][:].rearrange("m j u p e -> m j u (p e)").bitcast(F32)
                    turn_back(words[:, 2 * (c % 2) : 2 * (c % 2) + 2, :, :], x_chunks + c)
                for c in range(x_chunks):
                    turn_back(x_t[:, 2 * c : 2 * c + 2, :, :], c)
            if i == last - 1:
                banks = [("turn", 4)] * 4 + [("second", 2)] * 2 + [("first", 2)] * 2
                for j, (tag, bufs) in enumerate(banks):
                    e_banks[j] = psum.tile([P, NP], F32, name="e_bank", tag=tag, bufs=bufs)
                    compare(j, 0)

        quantise(x_w[1], x_s[1], 0, x_bf[:].rearrange("p n t -> p (n t)"))
        for c in range(page_chunks):
            weave_page(last, c)
            quantise(page_w[1], page_s[1], c, page_bf[c][:].rearrange("p m t -> p (m t)"))
        for j in range(TILES):
            compare(j, 1)
            store(j)
